import numpy as np
import ml_dtypes


def mxq(x, axis, fmt="e4m3"):
    dtype, down = {"e4m3": (ml_dtypes.float8_e4m3fn, 7), "e5m2": (ml_dtypes.float8_e5m2, 14)}[fmt]
    v = np.moveaxis(np.asarray(x, np.float32).astype(ml_dtypes.bfloat16).astype(np.float64), axis, -1)
    blocks = v.reshape(v.shape[:-1] + (-1, 32))
    amax = np.abs(blocks).max(-1, keepdims=True)
    byte = np.maximum(np.where(amax > 0, np.frexp(amax)[1] - 1 + 127, 0) - down, 1)
    scale = np.exp2(byte - 127.0)
    codes = (blocks / scale).astype(np.float32).astype(dtype).astype(np.float64)
    return np.moveaxis((codes * scale).reshape(v.shape), -1, axis)


WIDE = False


def mx_kscale(k):
    if not WIDE:
        return np.ones(k)
    levels = np.array([10, -10, 5, -5, 0])
    if k % 512:
        return np.exp2(np.random.permutation(np.resize(levels, k // 32))).repeat(32)
    a = np.empty((k // 512, 16))
    for p in range(k // 512):
        a[p, :8] = np.random.permutation(np.resize(levels, 8))
        for g in range(8):
            far = levels[np.abs(levels - a[p, g]) >= 10]
            a[p, g + 8] = far[np.random.randint(len(far))]
    return np.exp2(a.ravel()).repeat(32)


def f64(x):
    return np.asarray(x).astype(np.float64)


E2M1 = np.array([0.0, 0.5, 1.0, 1.5, 2.0, 3.0, 4.0, 6.0, -0.0, -0.5, -1.0, -1.5, -2.0, -3.0, -4.0, -6.0])


def pack_weight(w, fmt):
    k, n = w.shape
    w = f64(np.asarray(w, np.float32).astype(ml_dtypes.bfloat16)).reshape(k // 32, 32, n)
    amax = np.abs(w).max(1)
    if fmt == "e4m3":
        byte = np.frexp(amax)[1] - 1 + 127 - 7
    else:
        mant, ex = np.frexp(amax / 6.0)
        byte = np.where(mant > 0.5, ex, ex - 1) + 127
    byte = np.clip(np.where(amax > 0, byte, 1), 1, 254)
    scaled = (w * np.exp2(127.0 - byte)[:, None, :]).reshape(k, n).astype(np.float32)
    by_word = np.ascontiguousarray(scaled.reshape(k // 512, 128, 4, n).transpose(0, 1, 3, 2))
    if fmt == "e4m3":
        words = by_word.astype(ml_dtypes.float8_e4m3fn).view(np.uint8)
    else:
        c = by_word.astype(ml_dtypes.float4_e2m1fn).view(np.uint8) & 0xF
        words = (c[..., 0::2] | (c[..., 1::2] << 4)).reshape(k // 512, 128, 2 * n)
    return np.ascontiguousarray(words), np.ascontiguousarray(byte.astype(np.uint8).reshape(k // 512, 16, n))


def unpack_weight(words, scales, fmt):
    g, _, n = scales.shape
    words = np.ascontiguousarray(words).reshape(g, 128, n, -1)
    if fmt == "e4m3":
        vals = words.view(ml_dtypes.float8_e4m3fn).astype(np.float64)
    else:
        nib = np.empty((g, 128, n, 4), np.uint8)
        nib[..., 0::2] = words & 0xF
        nib[..., 1::2] = words >> 4
        vals = E2M1[nib]
    vals = vals * np.repeat(np.exp2(scales.astype(np.float64) - 127.0), 8, axis=1)[..., None]
    return vals.transpose(0, 1, 3, 2).reshape(g * 512, n)


K, M, T = 1024, 512, 1024


def setup_inputs():
    n = np.random.standard_normal
    s = mx_kscale(K)[:, None]
    p_wr = pack_weight(n((K, M)) / np.sqrt(K) / s, "e2m1")
    p_wk = pack_weight(n((K, M)) / np.sqrt(K) / s, "e4m3")
    return {
        "x": (np.round(32.0 * n((K, T + 1))) / 32.0 * s).astype(np.float32),
        "mu": (np.random.randint(1, 16, (K, 3)) / 16.0).astype(np.float32),
        "wr_words": p_wr[0],
        "wr_scales": p_wr[1],
        "wk_words": p_wk[0],
        "wk_scales": p_wk[1],
        "wv": (n((K, M)) / np.sqrt(K) / s).astype(np.float32),
    }


def reference(x, mu, wr_words, wr_scales, wk_words, wk_scales, wv):
    now, before = f64(x)[:, 1:], f64(x)[:, :-1]
    xr_, xk_, xv_ = [mxq(now + f64(mu)[:, i:i + 1] * (before - now), 0, "e4m3") for i in range(3)]
    wr_ = unpack_weight(wr_words, wr_scales, "e2m1")
    wk_ = unpack_weight(wk_words, wk_scales, "e4m3")
    wv_ = mxq(f64(wv), 0, "e4m3")
    return wr_.T @ xr_, wk_.T @ xk_, wv_.T @ xv_

@@ -1,0 +1,230 @@
+from contextlib import ExitStack
+
+import concourse.mybir as mybir
+
+K, M, T = 1024, 512, 1024
+FLOPS = 3 * 2 * K * M * T
+
+F32 = mybir.dt.float32
+BF16 = mybir.dt.bfloat16
+I32 = mybir.dt.int32
+U32 = mybir.dt.uint32
+U8 = mybir.dt.uint8
+FP8X4 = mybir.dt.float8_e4m3fn_x4
+FP4X4 = mybir.dt.float4_e2m1fn_x4
+ALU = mybir.AluOpType
+
+P = 128
+PACK = 4
+K_PASS = P * PACK
+PASSES = K // K_PASS
+N_TILES = M // P
+CHUNKS = [256, 512, 256]
+LEAD = 8
+QUANT_LAG = 2
+WV_STEPS = {0: (3, "scalar"), 1: (6, "vector")}
+WV_READY = 8
+
+
+def tile_mix_rwkv_fm_none_kernel(
+    tc, x, mu, wr_words, wr_scales, wk_words, wk_scales, wv, out_0, out_1, out_2
+):
+    nc = tc.nc
+    outs = [out_0, out_1, out_2]
+    starts = [sum(CHUNKS[:c]) for c in range(len(CHUNKS))]
+    units = [(c, i, a) for c in range(len(CHUNKS)) for i in range(3) for a in range(PASSES)]
+    last = len(units) - 1
+
+    with ExitStack() as ctx:
+        keep = ctx.enter_context(tc.tile_pool(name="keep", bufs=1))
+        work = ctx.enter_context(tc.tile_pool(name="work", bufs=4))
+        psum = ctx.enter_context(tc.psum_pool(name="psum", bufs=8))
+        ctx.enter_context(tc.manual_schedule())
+
+        mu_sb = keep.tile([P, PASSES, 16], F32, name="mu_sb")
+        wr_sb = keep.tile([P, PASSES, 2 * M], U8, name="wr_sb", align_bytes=64)
+        wk_sb = keep.tile([P, PASSES, M], U32, name="wk_sb", align_bytes=64)
+        wr_sc = keep.tile([P, PASSES, M], U8, name="wr_sc", align_bytes=64)
+        wk_sc = keep.tile([P, PASSES, M], U8, name="wk_sc", align_bytes=64)
+        wv_raw = [keep.tile([P, PACK, M], F32, name="wv_raw%d" % a) for a in range(PASSES)]
+        wv_bf = [keep.tile([P, M, PACK], BF16, name="wv_bf%d" % a, align_bytes=64) for a in range(PASSES)]
+        wv_q = [keep.tile([P, M], U32, name="wv_q%d" % a, align_bytes=64) for a in range(PASSES)]
+        wv_sc = [keep.tile([P, M], U8, name="wv_sc%d" % a, align_bytes=64) for a in range(PASSES)]
+        x_sb = {}
+        for c, width in enumerate(CHUNKS):
+            for a in range(PASSES):
+                x_sb[c, a] = keep.tile([P, PACK, LEAD + width], F32, name="x%d_%d" % (c, a))
+
+        def load_x(c, a):
+            rows = x[a * K_PASS : (a + 1) * K_PASS, starts[c] : starts[c] + CHUNKS[c] + 1]
+            nc.sync.dma_start(out=x_sb[c, a][:, :, LEAD - 1 :], in_=rows.rearrange("(p j) t -> p j t", j=PACK))
+
+        def load_scales(plane, scales):
+            words = scales.bitcast(I32)
+            for r in range(4):
+                nc.sync.dma_start(
+                    out=plane[:].bitcast(I32)[r:P:32, :, :],
+                    in_=words[:, r:16:4, :].rearrange("a q n -> q a n"),
+                )
+
+        def load_wv(a):
+            rows = wv[a * K_PASS : (a + 1) * K_PASS, :]
+            nc.sync.dma_start(out=wv_raw[a][:], in_=rows.rearrange("(p j) n -> p j n", j=PACK))
+
+        nc.vector.memset(wr_sc[:].bitcast(I32), 0)
+        nc.vector.memset(wk_sc[:].bitcast(I32), 0)
+
+        load_x(0, 0)
+        nc.sync.dma_start(out=mu_sb[:, :, : 3 * PACK], in_=mu.rearrange("(a p j) i -> p a (j i)", a=PASSES, j=PACK))
+        load_x(0, 1)
+        nc.sync.dma_start(out=wr_sb[:].bitcast(I32), in_=wr_words.rearrange("a p b -> p a b").bitcast(I32))
+        load_scales(wr_sc, wr_scales)
+        nc.sync.dma_start(out=wk_sb[:].bitcast(I32), in_=wk_words.rearrange("a p n t -> p a (n t)").bitcast(I32))
+        load_scales(wk_sc, wk_scales)
+        load_wv(0)
+        load_x(1, 0)
+        load_wv(1)
+        load_x(1, 1)
+        for c in range(2, len(CHUNKS)):
+            for a in range(PASSES):
+                load_x(c, a)
+
+        def interleave(engine, dst, src):
+            dst4 = dst.rearrange("p (c i) j -> p c j i", i=4)
+            src4 = src.rearrange("p j (c i) -> p c j i", i=4)
+            if engine == "scalar":
+                nc.scalar.copy(out=dst4, in_=src4)
+            else:
+                nc.vector.tensor_copy(out=dst4, in_=src4)
+
+        def quantize(codes, scales, grouped):
+            nc.vector.quantize_mx(out=codes.bitcast(FP8X4), scales=scales, in_=grouped.rearrange("p t j -> p (t j)"))
+
+        diff, rows_bf, grouped, codes, scales, acc, result = {}, {}, {}, {}, {}, {}, {}
+
+        def difference(c, a, pieces):
+            width = CHUNKS[c]
+            diff[c, a] = work.tile([P, PACK, width], F32, name="diff", tag="diff")
+            step = PACK // pieces
+            for j in range(0, PACK, step):
+                nc.vector.tensor_tensor(
+                    out=diff[c, a][:, j : j + step, :],
+                    in0=x_sb[c, a][:, j : j + step, LEAD - 1 : LEAD - 1 + width],
+                    in1=x_sb[c, a][:, j : j + step, LEAD:],
+                    op=ALU.subtract,
+                )
+
+        def blend(s):
+            c, i, a = units[s]
+            rows_bf[s] = work.tile([P, PACK, CHUNKS[c]], BF16, name="rows_bf", tag="rows_bf")
+            for j in range(PACK):
+                nc.vector.scalar_tensor_tensor(
+                    out=rows_bf[s][:, j, :],
+                    in0=diff[c, a][:, j, :],
+                    scalar=mu_sb[:, a, 3 * j + i : 3 * j + i + 1],
+                    in1=x_sb[c, a][:, j, LEAD:],
+                    op0=ALU.mult,
+                    op1=ALU.add,
+                )
+
+        def group_rows(s, engine):
+            grouped[s] = work.tile([P, CHUNKS[units[s][0]], PACK], BF16, name="grouped", tag="grouped", align_bytes=64)
+            interleave(engine, grouped[s][:], rows_bf[s][:])
+
+        def quantize_unit(s):
+            width = CHUNKS[units[s][0]]
+            codes[s] = work.tile([P, width], U32, name="codes", tag="codes", bufs=6, align_bytes=64)
+            scales[s] = work.tile([P, width], U8, name="scales", tag="scales", bufs=6, align_bytes=64)
+            quantize(codes[s][:], scales[s][:], grouped[s][:])
+
+        def weight(i, a, nt):
+            cols = slice(nt * P, (nt + 1) * P)
+            if i == 0:
+                return wr_sb[:, a, 2 * nt * P : 2 * (nt + 1) * P].bitcast(FP4X4), wr_sc[:, a, cols]
+            if i == 1:
+                return wk_sb[:, a, cols].bitcast(FP8X4), wk_sc[:, a, cols]
+            return wv_q[a][:, cols].bitcast(FP8X4), wv_sc[a][:, cols]
+
+        def one_pass(s, nt, cols):
+            c, i, a = units[s]
+            w_codes, w_scales = weight(i, a, nt)
+            nc.tensor.matmul_mx(
+                out=acc[c, i, nt][:, cols],
+                lhsT=w_codes,
+                lhsT_scale=w_scales,
+                rhs=codes[s][:, cols].bitcast(FP8X4),
+                rhs_scale=scales[s][:, cols],
+                start=(a == 0),
+                stop=(a == PASSES - 1),
+            )
+
+        def multiply(s):
+            c, i, a = units[s]
+            width = CHUNKS[c]
+            if a == 0:
+                for nt in range(N_TILES):
+                    acc[c, i, nt] = psum.tile([P, 512], F32, name="acc", tag="acc")
+            if i == 0 and width == 256:
+                if a == PASSES - 1:
+                    for nt in range(N_TILES):
+                        for t0 in range(0, width, P):
+                            for u in range(s - a, s + 1):
+                                one_pass(u, nt, slice(t0, t0 + P))
+            else:
+                for nt in range(N_TILES):
+                    one_pass(s, nt, slice(0, width))
+
+        def drain(c, i, nt, engine):
+            width = CHUNKS[c]
+            if nt % 2 == 0:
+                result[c, i, nt // 2] = work.tile([P, 2, width], F32, name="result", tag="result", bufs=8)
+            dst = result[c, i, nt // 2][:, nt % 2, :]
+            if engine == "scalar":
+                nc.scalar.copy(out=dst, in_=acc[c, i, nt][:, :width])
+            else:
+                nc.vector.tensor_copy(out=dst, in_=acc[c, i, nt][:, :width])
+            if nt % 2 == 1:
+                rows = outs[i][(nt - 1) * P : (nt + 1) * P, starts[c] : starts[c] + width]
+                nc.sync.dma_start(out=rows.rearrange("(h p) t -> p h t", p=P), in_=result[c, i, nt // 2][:])
+
+        to_multiply, to_drain = [], []
+        difference(0, 0, 2)
+        for s in range(len(units) + QUANT_LAG):
+            if s <= last:
+                blend(s)
+            if s + 1 <= last and units[s + 1][1] == 0:
+                difference(units[s + 1][0], units[s + 1][2], 2 if s < QUANT_LAG else 1)
+            for a in range(PASSES):
+                if WV_STEPS[a] == (s, "vector"):
+                    interleave("vector", wv_bf[a][:], wv_raw[a][:])
+            if s == last:
+                quantize_unit(s - QUANT_LAG)
+                to_multiply.append(s - QUANT_LAG)
+                group_rows(s, "vector")
+            elif s >= QUANT_LAG:
+                quantize_unit(s - QUANT_LAG)
+                to_multiply.append(s - QUANT_LAG)
+            for a in range(PASSES):
+                if WV_STEPS[a][0] + 1 == s - (WV_STEPS[a][1] == "scalar"):
+                    quantize(wv_q[a][:], wv_sc[a][:], wv_bf[a][:])
+            while to_multiply and (units[to_multiply[0]][1] < 2 or s >= WV_READY):
+                u = to_multiply[0]
+                to_multiply = to_multiply[1:]
+                multiply(u)
+                if units[u][2] == PASSES - 1:
+                    to_drain.extend((units[u][0], units[u][1], nt) for nt in range(N_TILES))
+            if s < last:
+                group_rows(s, "scalar")
+            for a in range(PASSES):
+                if WV_STEPS[a] == (s, "scalar"):
+                    interleave("scalar", wv_bf[a][:], wv_raw[a][:])
+            if s <= last:
+                for entry in to_drain[:2]:
+                    drain(entry[0], entry[1], entry[2], "scalar")
+                to_drain = to_drain[2:]
+            elif s == last + 1:
+                for entry in to_drain:
+                    drain(entry[0], entry[1], entry[2], "scalar")
+                to_drain = []
+        for entry in to_drain:
+            drain(entry[0], entry[1], entry[2], "scalar" if entry[2] < 2 else "vector")

@@ -20,10 +20,20 @@ K_PASS = P * PACK
 PASSES = K // K_PASS
 N_TILES = M // P
 CHUNKS = [256, 512, 256]
+PASS_MAJOR = [True, False, False]
 LEAD = 8
+TAIL = 128
 QUANT_LAG = 2
-WV_STEPS = {0: (3, "scalar"), 1: (6, "vector")}
-WV_READY = 8
+QUANT_EARLY = [15, 16, 17, 18]
+FIRST_SPLIT = 4
+LOADS = ["x00", "mu", "x01", "wv0", "x10", "wr", "wv1", "x11", "wk", "x20", "x21"]
+DIFF_LEAD = {(2, 0): 2, (1, 0): 2}
+WV_PIECES = [(0, 0, 1), (0, 1, 3), (1, 0, 4), (1, 1, 4)]
+WV_ON_VECTOR = []
+WV_QUANT = [4, 6]
+DRAINS = [0, 0, 0, 0, 0, 0, 4, 1, 1, 0, 3, 0, 2, 2, 3, 2, 4, 0, 4, 3, 2, 2]
+VECTOR_DRAINS = {}
+VECTOR_TOKENS = {14: 256, 15: 256, 17: 128, 18: 128}
 
 
 def tile_mix_rwkv_fm_none_kernel(
@@ -32,7 +42,16 @@ def tile_mix_rwkv_fm_none_kernel(
     nc = tc.nc
     outs = [out_0, out_1, out_2]
     starts = [sum(CHUNKS[:c]) for c in range(len(CHUNKS))]
-    units = [(c, i, a) for c in range(len(CHUNKS)) for i in range(3) for a in range(PASSES)]
+    units = []
+    for c in range(len(CHUNKS)):
+        if PASS_MAJOR[c]:
+            units.extend((c, i, a) for a in range(PASSES) for i in range(3))
+        else:
+            units.extend((c, i, a) for i in range(3) for a in range(PASSES))
+    spans = [slice(0, CHUNKS[c]) for c, i, a in units]
+    units.append(units[-1])
+    spans[-1:] = [slice(0, CHUNKS[-1] - TAIL), slice(CHUNKS[-1] - TAIL, CHUNKS[-1])]
+    widths = [span.stop - span.start for span in spans]
     last = len(units) - 1
 
     with ExitStack() as ctx:
@@ -55,9 +74,12 @@ def tile_mix_rwkv_fm_none_kernel(
             for a in range(PASSES):
                 x_sb[c, a] = keep.tile([P, PACK, LEAD + width], F32, name="x%d_%d" % (c, a))
 
-        def load_x(c, a):
+        def load_x(c, a, pieces):
             rows = x[a * K_PASS : (a + 1) * K_PASS, starts[c] : starts[c] + CHUNKS[c] + 1]
-            nc.sync.dma_start(out=x_sb[c, a][:, :, LEAD - 1 :], in_=rows.rearrange("(p j) t -> p j t", j=PACK))
+            rows = rows.rearrange("(p j) t -> p j t", j=PACK)
+            step = PACK // pieces
+            for j in range(0, PACK, step):
+                nc.sync.dma_start(out=x_sb[c, a][:, j : j + step, LEAD - 1 :], in_=rows[:, j : j + step, :])
 
         def load_scales(plane, scales):
             words = scales.bitcast(I32)
@@ -74,20 +96,23 @@ def tile_mix_rwkv_fm_none_kernel(
         nc.vector.memset(wr_sc[:].bitcast(I32), 0)
         nc.vector.memset(wk_sc[:].bitcast(I32), 0)
 
-        load_x(0, 0)
-        nc.sync.dma_start(out=mu_sb[:, :, : 3 * PACK], in_=mu.rearrange("(a p j) i -> p a (j i)", a=PASSES, j=PACK))
-        load_x(0, 1)
-        nc.sync.dma_start(out=wr_sb[:].bitcast(I32), in_=wr_words.rearrange("a p b -> p a b").bitcast(I32))
-        load_scales(wr_sc, wr_scales)
-        nc.sync.dma_start(out=wk_sb[:].bitcast(I32), in_=wk_words.rearrange("a p n t -> p a (n t)").bitcast(I32))
-        load_scales(wk_sc, wk_scales)
-        load_wv(0)
-        load_x(1, 0)
-        load_wv(1)
-        load_x(1, 1)
-        for c in range(2, len(CHUNKS)):
-            for a in range(PASSES):
-                load_x(c, a)
+        for what in LOADS:
+            if what == "mu":
+                nc.sync.dma_start(
+                    out=mu_sb[:, :, : 3 * PACK], in_=mu.rearrange("(a p j) i -> p a (j i)", a=PASSES, j=PACK)
+                )
+            elif what == "wr":
+                nc.sync.dma_start(out=wr_sb[:].bitcast(I32), in_=wr_words.rearrange("a p b -> p a b").bitcast(I32))
+                load_scales(wr_sc, wr_scales)
+            elif what == "wk":
+                nc.sync.dma_start(
+                    out=wk_sb[:].bitcast(I32), in_=wk_words.rearrange("a p n t -> p a (n t)").bitcast(I32)
+                )
+                load_scales(wk_sc, wk_scales)
+            elif what.startswith("wv"):
+                load_wv(int(what[2]))
+            else:
+                load_x(int(what[1]), int(what[2]), FIRST_SPLIT if what == "x00" else 1)
 
         def interleave(engine, dst, src):
             dst4 = dst.rearrange("p (c i) j -> p c j i", i=4)
@@ -100,7 +125,7 @@ def tile_mix_rwkv_fm_none_kernel(
         def quantize(codes, scales, grouped):
             nc.vector.quantize_mx(out=codes.bitcast(FP8X4), scales=scales, in_=grouped.rearrange("p t j -> p (t j)"))
 
-        diff, rows_bf, grouped, codes, scales, acc, result = {}, {}, {}, {}, {}, {}, {}
+        diff, rows_bf, grouped, codes, scales, acc = {}, {}, {}, {}, {}, {}
 
         def difference(c, a, pieces):
             width = CHUNKS[c]
@@ -116,25 +141,30 @@ def tile_mix_rwkv_fm_none_kernel(
 
         def blend(s):
             c, i, a = units[s]
-            rows_bf[s] = work.tile([P, PACK, CHUNKS[c]], BF16, name="rows_bf", tag="rows_bf")
+            rows_bf[s] = work.tile([P, PACK, widths[s]], BF16, name="rows_bf", tag="rows_bf")
             for j in range(PACK):
                 nc.vector.scalar_tensor_tensor(
                     out=rows_bf[s][:, j, :],
-                    in0=diff[c, a][:, j, :],
+                    in0=diff[c, a][:, j, spans[s]],
                     scalar=mu_sb[:, a, 3 * j + i : 3 * j + i + 1],
-                    in1=x_sb[c, a][:, j, LEAD:],
+                    in1=x_sb[c, a][:, j, LEAD:][:, spans[s]],
                     op0=ALU.mult,
                     op1=ALU.add,
                 )
 
         def group_rows(s, engine):
-            grouped[s] = work.tile([P, CHUNKS[units[s][0]], PACK], BF16, name="grouped", tag="grouped", align_bytes=64)
-            interleave(engine, grouped[s][:], rows_bf[s][:])
+            width = widths[s]
+            if s not in grouped:
+                grouped[s] = work.tile([P, width, PACK], BF16, name="grouped", tag="grouped", align_bytes=64)
+            cut = min(VECTOR_TOKENS.get(s, 0), width)
+            cols = slice(0, cut) if engine == "vector" else slice(cut, width)
+            if cols.stop > cols.start:
+                interleave(engine, grouped[s][:, cols, :], rows_bf[s][:, :, cols])
 
         def quantize_unit(s):
-            width = CHUNKS[units[s][0]]
-            codes[s] = work.tile([P, width], U32, name="codes", tag="codes", bufs=6, align_bytes=64)
-            scales[s] = work.tile([P, width], U8, name="scales", tag="scales", bufs=6, align_bytes=64)
+            width = widths[s]
+            codes[s] = work.tile([P, width], U32, name="codes", tag="codes", bufs=10, align_bytes=64)
+            scales[s] = work.tile([P, width], U8, name="scales", tag="scales", bufs=10, align_bytes=64)
             quantize(codes[s][:], scales[s][:], grouped[s][:])
 
         def weight(i, a, nt):
@@ -145,11 +175,11 @@ def tile_mix_rwkv_fm_none_kernel(
                 return wk_sb[:, a, cols].bitcast(FP8X4), wk_sc[:, a, cols]
             return wv_q[a][:, cols].bitcast(FP8X4), wv_sc[a][:, cols]
 
-        def one_pass(s, nt, cols):
+        def one_pass(s, nt, dst, cols):
             c, i, a = units[s]
             w_codes, w_scales = weight(i, a, nt)
             nc.tensor.matmul_mx(
-                out=acc[c, i, nt][:, cols],
+                out=dst,
                 lhsT=w_codes,
                 lhsT_scale=w_scales,
                 rhs=codes[s][:, cols].bitcast(FP8X4),
@@ -160,71 +190,84 @@ def tile_mix_rwkv_fm_none_kernel(
 
         def multiply(s):
             c, i, a = units[s]
-            width = CHUNKS[c]
-            if a == 0:
+            width = widths[s]
+            if s == last - 2:
                 for nt in range(N_TILES):
-                    acc[c, i, nt] = psum.tile([P, 512], F32, name="acc", tag="acc")
-            if i == 0 and width == 256:
-                if a == PASSES - 1:
-                    for nt in range(N_TILES):
-                        for t0 in range(0, width, P):
-                            for u in range(s - a, s + 1):
-                                one_pass(u, nt, slice(t0, t0 + P))
-            else:
+                    acc[last, nt] = psum.tile([P, 512], F32, name="acc", tag="acc")
+                    one_pass(s, nt, acc[last, nt][:, :TAIL], spans[last])
+                return []
+            if s == last:
                 for nt in range(N_TILES):
-                    one_pass(s, nt, slice(0, width))
+                    one_pass(s, nt, acc[last, nt][:, :TAIL], slice(0, TAIL))
+                return [(s, nt, 1) for nt in range(N_TILES)]
+            if a < PASSES - 1:
+                return []
+            per_bank = 512 // width
+            n_cols = P if i == 0 and width < 512 else width
+            for nt in range(N_TILES):
+                if nt % per_bank == 0:
+                    acc[s, nt] = psum.tile([P, 512], F32, name="acc", tag="acc")
+                bank = acc[s, nt - nt % per_bank]
+                for t0 in range(0, width, n_cols):
+                    at = (nt % per_bank) * width + t0
+                    for b in range(PASSES):
+                        one_pass(units.index((c, i, b)), nt, bank[:, at : at + n_cols], slice(t0, t0 + n_cols))
+            return [(s, nt, per_bank) for nt in range(0, N_TILES, per_bank)]
 
-        def drain(c, i, nt, engine):
-            width = CHUNKS[c]
-            if nt % 2 == 0:
-                result[c, i, nt // 2] = work.tile([P, 2, width], F32, name="result", tag="result", bufs=8)
-            dst = result[c, i, nt // 2][:, nt % 2, :]
+        def drain(entry, engine):
+            s, nt, count = entry
+            c, i, a = units[s]
+            width = widths[s]
+            t0 = starts[c] + spans[s].start
+            result = work.tile([P, count, width], F32, name="result", tag="result", bufs=12)
+            src = acc[s, nt][:, : count * width].rearrange("p (h t) -> p h t", h=count)
             if engine == "scalar":
-                nc.scalar.copy(out=dst, in_=acc[c, i, nt][:, :width])
+                nc.scalar.copy(out=result[:], in_=src)
             else:
-                nc.vector.tensor_copy(out=dst, in_=acc[c, i, nt][:, :width])
-            if nt % 2 == 1:
-                rows = outs[i][(nt - 1) * P : (nt + 1) * P, starts[c] : starts[c] + width]
-                nc.sync.dma_start(out=rows.rearrange("(h p) t -> p h t", p=P), in_=result[c, i, nt // 2][:])
+                nc.vector.tensor_copy(out=result[:], in_=src)
+            rows = outs[i][nt * P : (nt + count) * P, t0 : t0 + width]
+            nc.sync.dma_start(out=rows.rearrange("(h p) t -> p h t", p=P), in_=result[:])
+
+        def convert_wv(s, engine):
+            for n, (a, h, at) in enumerate(WV_PIECES):
+                if at == s and (n in WV_ON_VECTOR) == (engine == "vector"):
+                    cols = slice(h * M // 2, (h + 1) * M // 2)
+                    interleave(engine, wv_bf[a][:, cols, :], wv_raw[a][:, :, cols])
+
+        diff_at = {}
+        for c in range(len(CHUNKS)):
+            for a in range(PASSES):
+                diff_at.setdefault(units.index((c, 0, a)) - DIFF_LEAD.get((c, a), 1), []).append((c, a))
 
         to_multiply, to_drain = [], []
-        difference(0, 0, 2)
+        difference(0, 0, FIRST_SPLIT)
         for s in range(len(units) + QUANT_LAG):
             if s <= last:
                 blend(s)
-            if s + 1 <= last and units[s + 1][1] == 0:
-                difference(units[s + 1][0], units[s + 1][2], 2 if s < QUANT_LAG else 1)
-            for a in range(PASSES):
-                if WV_STEPS[a] == (s, "vector"):
-                    interleave("vector", wv_bf[a][:], wv_raw[a][:])
-            if s == last:
-                quantize_unit(s - QUANT_LAG)
-                to_multiply.append(s - QUANT_LAG)
-                group_rows(s, "vector")
-            elif s >= QUANT_LAG:
-                quantize_unit(s - QUANT_LAG)
-                to_multiply.append(s - QUANT_LAG)
-            for a in range(PASSES):
-                if WV_STEPS[a][0] + 1 == s - (WV_STEPS[a][1] == "scalar"):
-                    quantize(wv_q[a][:], wv_sc[a][:], wv_bf[a][:])
-            while to_multiply and (units[to_multiply[0]][1] < 2 or s >= WV_READY):
-                u = to_multiply[0]
-                to_multiply = to_multiply[1:]
-                multiply(u)
-                if units[u][2] == PASSES - 1:
-                    to_drain.extend((units[u][0], units[u][1], nt) for nt in range(N_TILES))
-            if s < last:
-                group_rows(s, "scalar")
-            for a in range(PASSES):
-                if WV_STEPS[a] == (s, "scalar"):
-                    interleave("scalar", wv_bf[a][:], wv_raw[a][:])
+            for c, a in diff_at.get(s, []):
+                difference(c, a, 2 if s < QUANT_LAG else 1)
+            convert_wv(s, "vector")
+            for u in range(max(s - QUANT_LAG, 0), min(s, len(units))):
+                if u not in codes and (u == s - QUANT_LAG or u in QUANT_EARLY):
+                    quantize_unit(u)
+                    to_multiply.append(u)
             if s <= last:
-                for entry in to_drain[:2]:
-                    drain(entry[0], entry[1], entry[2], "scalar")
-                to_drain = to_drain[2:]
-            elif s == last + 1:
-                for entry in to_drain:
-                    drain(entry[0], entry[1], entry[2], "scalar")
-                to_drain = []
-        for entry in to_drain:
-            drain(entry[0], entry[1], entry[2], "scalar" if entry[2] < 2 else "vector")
+                group_rows(s, "vector")
+            for a in range(PASSES):
+                if WV_QUANT[a] == s:
+                    quantize(wv_q[a][:], wv_sc[a][:], wv_bf[a][:])
+            while to_multiply and (units[to_multiply[0]][1] < 2 or s >= max(WV_QUANT)):
+                to_drain.extend(multiply(to_multiply[0]))
+                to_multiply = to_multiply[1:]
+            if s <= last:
+                group_rows(s, "scalar")
+            convert_wv(s, "scalar")
+            if s < len(units) + QUANT_LAG - 1:
+                for entry in to_drain[: DRAINS[s]]:
+                    drain(entry, "scalar")
+                to_drain = to_drain[DRAINS[s] :]
+                for entry in to_drain[: VECTOR_DRAINS.get(s, 0)]:
+                    drain(entry, "vector")
+                to_drain = to_drain[VECTOR_DRAINS.get(s, 0) :]
+        for n, entry in enumerate(to_drain):
+            drain(entry, "scalar" if n % 2 == 0 else "vector")

@@ -13,27 +13,29 @@ U8 = mybir.dt.uint8
 FP8X4 = mybir.dt.float8_e4m3fn_x4
 FP4X4 = mybir.dt.float4_e2m1fn_x4
 ALU = mybir.AluOpType
+ACT = mybir.ActivationFunctionType
 
 P = 128
-PACK = 4
-K_PASS = P * PACK
+SLOTS = 4
+K_PASS = P * SLOTS
 PASSES = K // K_PASS
+BLENDS = 3
+V_BLEND = 2
 N_TILES = M // P
+BANK = 512
+MU_PITCH = 16
+PAD = 8
+
 CHUNKS = [256, 512, 256]
-PASS_MAJOR = [True, False, False]
-LEAD = 8
-TAIL = 128
+SCALED_SLOTS = {(0, 0): 4, (1, 0): 1}
+SCALE_LEAD = 2
 QUANT_LAG = 2
-QUANT_EARLY = [15, 16, 17, 18]
-FIRST_SPLIT = 4
-LOADS = ["x00", "mu", "x01", "wv0", "x10", "wr", "wv1", "x11", "wk", "x20", "x21"]
-DIFF_LEAD = {(2, 0): 2, (1, 0): 2}
-WV_PIECES = [(0, 0, 1), (0, 1, 3), (1, 0, 4), (1, 1, 4)]
-WV_ON_VECTOR = []
-WV_QUANT = [4, 6]
-DRAINS = [0, 0, 0, 0, 0, 0, 4, 1, 1, 0, 3, 0, 2, 2, 3, 2, 4, 0, 4, 3, 2, 2]
-VECTOR_DRAINS = {}
-VECTOR_TOKENS = {14: 256, 15: 256, 17: 128, 18: 128}
+LATE_UNITS = 3
+SHARED_UNITS = 5
+SHARED_TOKENS = 128
+WV_CAST_FROM = 2
+WV_QUANT_STEPS = [5, 7]
+DRAINS_PER_STEP = 3
 
 
 def tile_mix_rwkv_fm_none_kernel(
@@ -42,16 +44,9 @@ def tile_mix_rwkv_fm_none_kernel(
     nc = tc.nc
     outs = [out_0, out_1, out_2]
     starts = [sum(CHUNKS[:c]) for c in range(len(CHUNKS))]
-    units = []
-    for c in range(len(CHUNKS)):
-        if PASS_MAJOR[c]:
-            units.extend((c, i, a) for a in range(PASSES) for i in range(3))
-        else:
-            units.extend((c, i, a) for i in range(3) for a in range(PASSES))
-    spans = [slice(0, CHUNKS[c]) for c, i, a in units]
-    units.append(units[-1])
-    spans[-1:] = [slice(0, CHUNKS[-1] - TAIL), slice(CHUNKS[-1] - TAIL, CHUNKS[-1])]
-    widths = [span.stop - span.start for span in spans]
+
+    units = [(0, i, a) for a in range(PASSES) for i in range(BLENDS)]
+    units.extend((c, i, a) for c in range(1, len(CHUNKS)) for i in range(BLENDS) for a in range(PASSES))
     last = len(units) - 1
 
     with ExitStack() as ctx:
@@ -60,214 +55,226 @@ def tile_mix_rwkv_fm_none_kernel(
         psum = ctx.enter_context(tc.psum_pool(name="psum", bufs=8))
         ctx.enter_context(tc.manual_schedule())
 
-        mu_sb = keep.tile([P, PASSES, 16], F32, name="mu_sb")
-        wr_sb = keep.tile([P, PASSES, 2 * M], U8, name="wr_sb", align_bytes=64)
-        wk_sb = keep.tile([P, PASSES, M], U32, name="wk_sb", align_bytes=64)
-        wr_sc = keep.tile([P, PASSES, M], U8, name="wr_sc", align_bytes=64)
-        wk_sc = keep.tile([P, PASSES, M], U8, name="wk_sc", align_bytes=64)
-        wv_raw = [keep.tile([P, PACK, M], F32, name="wv_raw%d" % a) for a in range(PASSES)]
-        wv_bf = [keep.tile([P, M, PACK], BF16, name="wv_bf%d" % a, align_bytes=64) for a in range(PASSES)]
-        wv_q = [keep.tile([P, M], U32, name="wv_q%d" % a, align_bytes=64) for a in range(PASSES)]
-        wv_sc = [keep.tile([P, M], U8, name="wv_sc%d" % a, align_bytes=64) for a in range(PASSES)]
+        mu_sb = keep.tile([P, PASSES, MU_PITCH], F32, name="mu_sb")
+        rest_sb = keep.tile([P, PASSES, MU_PITCH], F32, name="rest_sb")
+        wr_codes = keep.tile([P, PASSES, 2 * M], U8, name="wr_codes", align_bytes=64)
+        wk_codes = keep.tile([P, PASSES, M], U32, name="wk_codes", align_bytes=64)
+        wr_plane = keep.tile([P, PASSES, M], U8, name="wr_plane", align_bytes=64)
+        wk_plane = keep.tile([P, PASSES, M], U8, name="wk_plane", align_bytes=64)
+        wv_rows = [keep.tile([P, SLOTS, M], F32, name="wv_rows%d" % a) for a in range(PASSES)]
+        wv_grouped = [keep.tile([P, M, SLOTS], BF16, name="wv_grouped%d" % a, align_bytes=64) for a in range(PASSES)]
+        wv_codes = [keep.tile([P, M], U32, name="wv_codes%d" % a, align_bytes=64) for a in range(PASSES)]
+        wv_plane = [keep.tile([P, M], U8, name="wv_plane%d" % a, align_bytes=64) for a in range(PASSES)]
         x_sb = {}
         for c, width in enumerate(CHUNKS):
             for a in range(PASSES):
-                x_sb[c, a] = keep.tile([P, PACK, LEAD + width], F32, name="x%d_%d" % (c, a))
+                x_sb[c, a] = keep.tile([P, SLOTS, PAD + width], F32, name="x%d_%d" % (c, a))
 
-        def load_x(c, a, pieces):
+        def load_x(c, a, slots_per_dma):
             rows = x[a * K_PASS : (a + 1) * K_PASS, starts[c] : starts[c] + CHUNKS[c] + 1]
-            rows = rows.rearrange("(p j) t -> p j t", j=PACK)
-            step = PACK // pieces
-            for j in range(0, PACK, step):
-                nc.sync.dma_start(out=x_sb[c, a][:, j : j + step, LEAD - 1 :], in_=rows[:, j : j + step, :])
-
-        def load_scales(plane, scales):
-            words = scales.bitcast(I32)
-            for r in range(4):
-                nc.sync.dma_start(
-                    out=plane[:].bitcast(I32)[r:P:32, :, :],
-                    in_=words[:, r:16:4, :].rearrange("a q n -> q a n"),
-                )
+            rows = rows.rearrange("(p j) t -> p j t", j=SLOTS)
+            for j in range(0, SLOTS, slots_per_dma):
+                slots = slice(j, j + slots_per_dma)
+                nc.sync.dma_start(out=x_sb[c, a][:, slots, PAD - 1 :], in_=rows[:, slots, :])
 
         def load_wv(a):
             rows = wv[a * K_PASS : (a + 1) * K_PASS, :]
-            nc.sync.dma_start(out=wv_raw[a][:], in_=rows.rearrange("(p j) n -> p j n", j=PACK))
+            nc.sync.dma_start(out=wv_rows[a][:], in_=rows.rearrange("(p j) n -> p j n", j=SLOTS))
 
-        nc.vector.memset(wr_sc[:].bitcast(I32), 0)
-        nc.vector.memset(wk_sc[:].bitcast(I32), 0)
-
-        for what in LOADS:
-            if what == "mu":
+        def load_packed(codes_sb, words, plane, scale_rows):
+            nc.sync.dma_start(out=codes_sb[:].bitcast(I32), in_=words.bitcast(I32))
+            for r in range(4):
                 nc.sync.dma_start(
-                    out=mu_sb[:, :, : 3 * PACK], in_=mu.rearrange("(a p j) i -> p a (j i)", a=PASSES, j=PACK)
-                )
-            elif what == "wr":
-                nc.sync.dma_start(out=wr_sb[:].bitcast(I32), in_=wr_words.rearrange("a p b -> p a b").bitcast(I32))
-                load_scales(wr_sc, wr_scales)
-            elif what == "wk":
-                nc.sync.dma_start(
-                    out=wk_sb[:].bitcast(I32), in_=wk_words.rearrange("a p n t -> p a (n t)").bitcast(I32)
-                )
-                load_scales(wk_sc, wk_scales)
-            elif what.startswith("wv"):
-                load_wv(int(what[2]))
-            else:
-                load_x(int(what[1]), int(what[2]), FIRST_SPLIT if what == "x00" else 1)
-
-        def interleave(engine, dst, src):
-            dst4 = dst.rearrange("p (c i) j -> p c j i", i=4)
-            src4 = src.rearrange("p j (c i) -> p c j i", i=4)
-            if engine == "scalar":
-                nc.scalar.copy(out=dst4, in_=src4)
-            else:
-                nc.vector.tensor_copy(out=dst4, in_=src4)
-
-        def quantize(codes, scales, grouped):
-            nc.vector.quantize_mx(out=codes.bitcast(FP8X4), scales=scales, in_=grouped.rearrange("p t j -> p (t j)"))
-
-        diff, rows_bf, grouped, codes, scales, acc = {}, {}, {}, {}, {}, {}
-
-        def difference(c, a, pieces):
-            width = CHUNKS[c]
-            diff[c, a] = work.tile([P, PACK, width], F32, name="diff", tag="diff")
-            step = PACK // pieces
-            for j in range(0, PACK, step):
-                nc.vector.tensor_tensor(
-                    out=diff[c, a][:, j : j + step, :],
-                    in0=x_sb[c, a][:, j : j + step, LEAD - 1 : LEAD - 1 + width],
-                    in1=x_sb[c, a][:, j : j + step, LEAD:],
-                    op=ALU.subtract,
+                    out=plane[:].bitcast(I32)[r:P:32, :, :],
+                    in_=scale_rows.bitcast(I32)[:, r:16:4, :].rearrange("a q n -> q a n"),
                 )
 
-        def blend(s):
-            c, i, a = units[s]
-            rows_bf[s] = work.tile([P, PACK, widths[s]], BF16, name="rows_bf", tag="rows_bf")
-            for j in range(PACK):
+        nc.vector.memset(wr_plane[:].bitcast(I32), 0)
+        nc.vector.memset(wk_plane[:].bitcast(I32), 0)
+
+        nc.sync.dma_start(
+            out=mu_sb[:, :, : BLENDS * SLOTS], in_=mu.rearrange("(a p j) i -> p a (j i)", a=PASSES, j=SLOTS)
+        )
+        load_x(0, 0, 1)
+        load_x(0, 1, SLOTS)
+        load_wv(0)
+        load_x(1, 0, SLOTS)
+        load_wv(1)
+        load_packed(wr_codes, wr_words.rearrange("a p b -> p a b"), wr_plane, wr_scales)
+        load_x(1, 1, SLOTS)
+        load_packed(wk_codes, wk_words.rearrange("a p n i -> p a (n i)"), wk_plane, wk_scales)
+        load_x(2, 0, SLOTS)
+        load_x(2, 1, SLOTS)
+
+        nc.vector.tensor_scalar(
+            out=rest_sb[:, :, : BLENDS * SLOTS],
+            in0=mu_sb[:, :, : BLENDS * SLOTS],
+            scalar1=-1.0,
+            scalar2=1.0,
+            op0=ALU.mult,
+            op1=ALU.add,
+        )
+
+        diff, scaled, blended, grouped, codes, planes, acc = {}, {}, {}, {}, {}, {}, {}
+
+        def before(c, a):
+            return x_sb[c, a][:, :, PAD - 1 : PAD - 1 + CHUNKS[c]]
+
+        def now(c, a):
+            return x_sb[c, a][:, :, PAD:]
+
+        def difference(c, a):
+            first = SCALED_SLOTS.get((c, a), 0)
+            diff[c, a] = work.tile([P, SLOTS, CHUNKS[c]], F32, name="diff", tag="diff")
+            nc.vector.tensor_tensor(
+                out=diff[c, a][:, first:, :],
+                in0=before(c, a)[:, first:, :],
+                in1=now(c, a)[:, first:, :],
+                op=ALU.subtract,
+            )
+
+        def scale_now(u):
+            c, i, a = units[u]
+            slots = SCALED_SLOTS[c, a]
+            scaled[u] = work.tile([P, slots, CHUNKS[c]], F32, name="scaled", tag="scaled")
+            for j in range(slots):
+                nc.scalar.activation(
+                    out=scaled[u][:, j, :],
+                    in_=now(c, a)[:, j, :],
+                    func=ACT.Copy,
+                    scale=rest_sb[:, a, BLENDS * j + i : BLENDS * j + i + 1],
+                )
+
+        def blend(u):
+            c, i, a = units[u]
+            first = SCALED_SLOTS.get((c, a), 0)
+            blended[u] = work.tile([P, SLOTS, CHUNKS[c]], BF16, name="blended", tag="blended")
+            for j in list(range(first, SLOTS)) + list(range(first)):
+                factor, term = (before(c, a), scaled[u]) if j < first else (diff[c, a], now(c, a))
                 nc.vector.scalar_tensor_tensor(
-                    out=rows_bf[s][:, j, :],
-                    in0=diff[c, a][:, j, spans[s]],
-                    scalar=mu_sb[:, a, 3 * j + i : 3 * j + i + 1],
-                    in1=x_sb[c, a][:, j, LEAD:][:, spans[s]],
+                    out=blended[u][:, j, :],
+                    in0=factor[:, j, :],
+                    scalar=mu_sb[:, a, BLENDS * j + i : BLENDS * j + i + 1],
+                    in1=term[:, j, :],
                     op0=ALU.mult,
                     op1=ALU.add,
                 )
 
-        def group_rows(s, engine):
-            width = widths[s]
-            if s not in grouped:
-                grouped[s] = work.tile([P, width, PACK], BF16, name="grouped", tag="grouped", align_bytes=64)
-            cut = min(VECTOR_TOKENS.get(s, 0), width)
-            cols = slice(0, cut) if engine == "vector" else slice(cut, width)
-            if cols.stop > cols.start:
-                interleave(engine, grouped[s][:, cols, :], rows_bf[s][:, :, cols])
+        def vector_tokens(u):
+            return SHARED_TOKENS if u > last - SHARED_UNITS else 0
 
-        def quantize_unit(s):
-            width = widths[s]
-            codes[s] = work.tile([P, width], U32, name="codes", tag="codes", bufs=10, align_bytes=64)
-            scales[s] = work.tile([P, width], U8, name="scales", tag="scales", bufs=10, align_bytes=64)
-            quantize(codes[s][:], scales[s][:], grouped[s][:])
+        def interleave_on_vector(u):
+            cut = vector_tokens(u)
+            nc.vector.tensor_copy(out=grouped[u][:, :cut, :], in_=blended[u][:, :, :cut].rearrange("p j t -> p t j"))
+
+        def interleave_on_scalar(u):
+            cut = vector_tokens(u)
+            nc.scalar.copy(
+                out=grouped[u][:, cut:, :].rearrange("p (g t) j -> p g j t", t=4),
+                in_=blended[u][:, :, cut:].rearrange("p j (g t) -> p g j t", t=4),
+            )
+
+        def cast_wv(piece):
+            a, half = divmod(piece, 2)
+            cols = slice(half * M // 2, (half + 1) * M // 2)
+            nc.scalar.copy(out=wv_grouped[a][:, cols, :], in_=wv_rows[a][:, :, cols].rearrange("p j n -> p n j"))
+
+        def quantize(codes_out, plane_out, source):
+            nc.vector.quantize_mx(
+                out=codes_out[:].bitcast(FP8X4), scales=plane_out[:], in_=source[:].rearrange("p t j -> p (t j)")
+            )
+
+        def quantize_unit(u):
+            width = CHUNKS[units[u][0]]
+            codes[u] = work.tile([P, width], U32, name="codes", tag="codes", bufs=10, align_bytes=64)
+            planes[u] = work.tile([P, width], U8, name="plane", tag="plane", bufs=10, align_bytes=64)
+            quantize(codes[u], planes[u], grouped[u])
 
         def weight(i, a, nt):
             cols = slice(nt * P, (nt + 1) * P)
             if i == 0:
-                return wr_sb[:, a, 2 * nt * P : 2 * (nt + 1) * P].bitcast(FP4X4), wr_sc[:, a, cols]
+                return wr_codes[:, a, 2 * nt * P : 2 * (nt + 1) * P].bitcast(FP4X4), wr_plane[:, a, cols]
             if i == 1:
-                return wk_sb[:, a, cols].bitcast(FP8X4), wk_sc[:, a, cols]
-            return wv_q[a][:, cols].bitcast(FP8X4), wv_sc[a][:, cols]
+                return wk_codes[:, a, cols].bitcast(FP8X4), wk_plane[:, a, cols]
+            return wv_codes[a][:, cols].bitcast(FP8X4), wv_plane[a][:, cols]
 
-        def one_pass(s, nt, dst, cols):
-            c, i, a = units[s]
-            w_codes, w_scales = weight(i, a, nt)
+        def one_pass(u, nt, sums, cols):
+            c, i, a = units[u]
+            w_codes, w_plane = weight(i, a, nt)
             nc.tensor.matmul_mx(
-                out=dst,
+                out=sums,
                 lhsT=w_codes,
-                lhsT_scale=w_scales,
-                rhs=codes[s][:, cols].bitcast(FP8X4),
-                rhs_scale=scales[s][:, cols],
+                lhsT_scale=w_plane,
+                rhs=codes[u][:, cols].bitcast(FP8X4),
+                rhs_scale=planes[u][:, cols],
                 start=(a == 0),
                 stop=(a == PASSES - 1),
             )
 
-        def multiply(s):
-            c, i, a = units[s]
-            width = widths[s]
-            if s == last - 2:
+        def multiply(u):
+            c, i, a = units[u]
+            width = CHUNKS[c]
+            if (c, i) == units[last][:2]:
                 for nt in range(N_TILES):
-                    acc[last, nt] = psum.tile([P, 512], F32, name="acc", tag="acc")
-                    one_pass(s, nt, acc[last, nt][:, :TAIL], spans[last])
-                return []
-            if s == last:
-                for nt in range(N_TILES):
-                    one_pass(s, nt, acc[last, nt][:, :TAIL], slice(0, TAIL))
-                return [(s, nt, 1) for nt in range(N_TILES)]
+                    if a == 0:
+                        acc[c, i, nt] = psum.tile([P, BANK], F32, name="acc", tag="acc")
+                    one_pass(u, nt, acc[c, i, nt][:, :width], slice(0, width))
+                return [(c, i, nt, 1) for nt in range(N_TILES)] if a == PASSES - 1 else []
             if a < PASSES - 1:
                 return []
-            per_bank = 512 // width
-            n_cols = P if i == 0 and width < 512 else width
+            per_bank = BANK // width
+            n_cols = P if i == 0 and width < BANK else width
             for nt in range(N_TILES):
                 if nt % per_bank == 0:
-                    acc[s, nt] = psum.tile([P, 512], F32, name="acc", tag="acc")
-                bank = acc[s, nt - nt % per_bank]
+                    acc[c, i, nt] = psum.tile([P, BANK], F32, name="acc", tag="acc")
+                bank = acc[c, i, nt - nt % per_bank]
                 for t0 in range(0, width, n_cols):
                     at = (nt % per_bank) * width + t0
                     for b in range(PASSES):
                         one_pass(units.index((c, i, b)), nt, bank[:, at : at + n_cols], slice(t0, t0 + n_cols))
-            return [(s, nt, per_bank) for nt in range(0, N_TILES, per_bank)]
+            return [(c, i, nt, per_bank) for nt in range(0, N_TILES, per_bank)]
 
-        def drain(entry, engine):
-            s, nt, count = entry
-            c, i, a = units[s]
-            width = widths[s]
-            t0 = starts[c] + spans[s].start
-            result = work.tile([P, count, width], F32, name="result", tag="result", bufs=12)
-            src = acc[s, nt][:, : count * width].rearrange("p (h t) -> p h t", h=count)
-            if engine == "scalar":
-                nc.scalar.copy(out=result[:], in_=src)
-            else:
-                nc.vector.tensor_copy(out=result[:], in_=src)
-            rows = outs[i][nt * P : (nt + count) * P, t0 : t0 + width]
+        def drain(finished, copy):
+            c, i, nt, tiles = finished
+            width = CHUNKS[c]
+            result = work.tile([P, tiles, width], F32, name="result", tag="result", bufs=12)
+            copy(out=result[:], in_=acc[c, i, nt][:, : tiles * width].rearrange("p (h t) -> p h t", h=tiles))
+            rows = outs[i][nt * P : (nt + tiles) * P, starts[c] : starts[c] + width]
             nc.sync.dma_start(out=rows.rearrange("(h p) t -> p h t", p=P), in_=result[:])
 
-        def convert_wv(s, engine):
-            for n, (a, h, at) in enumerate(WV_PIECES):
-                if at == s and (n in WV_ON_VECTOR) == (engine == "vector"):
-                    cols = slice(h * M // 2, (h + 1) * M // 2)
-                    interleave(engine, wv_bf[a][:, cols, :], wv_raw[a][:, :, cols])
-
-        diff_at = {}
-        for c in range(len(CHUNKS)):
-            for a in range(PASSES):
-                diff_at.setdefault(units.index((c, 0, a)) - DIFF_LEAD.get((c, a), 1), []).append((c, a))
+        needs_scaling = [u for u in range(len(units)) if (units[u][0], units[u][2]) in SCALED_SLOTS]
+        for u in range(SCALE_LEAD):
+            scale_now(u)
 
         to_multiply, to_drain = [], []
-        difference(0, 0, FIRST_SPLIT)
-        for s in range(len(units) + QUANT_LAG):
+        for s in range(len(units) + 1):
             if s <= last:
                 blend(s)
-            for c, a in diff_at.get(s, []):
-                difference(c, a, 2 if s < QUANT_LAG else 1)
-            convert_wv(s, "vector")
-            for u in range(max(s - QUANT_LAG, 0), min(s, len(units))):
-                if u not in codes and (u == s - QUANT_LAG or u in QUANT_EARLY):
+                grouped[s] = work.tile([P, CHUNKS[units[s][0]], SLOTS], BF16, name="grouped", tag="grouped", align_bytes=64)
+            if s < last and units[s + 1][1] == 0:
+                difference(units[s + 1][0], units[s + 1][2])
+            for u in range(max(s - QUANT_LAG, 0), s):
+                if u not in codes and (u == s - QUANT_LAG or u > last - LATE_UNITS):
                     quantize_unit(u)
                     to_multiply.append(u)
-            if s <= last:
-                group_rows(s, "vector")
-            for a in range(PASSES):
-                if WV_QUANT[a] == s:
-                    quantize(wv_q[a][:], wv_sc[a][:], wv_bf[a][:])
-            while to_multiply and (units[to_multiply[0]][1] < 2 or s >= max(WV_QUANT)):
+            if s <= last and vector_tokens(s):
+                interleave_on_vector(s)
+            if s in WV_QUANT_STEPS:
+                a = WV_QUANT_STEPS.index(s)
+                quantize(wv_codes[a], wv_plane[a], wv_grouped[a])
+            while to_multiply and (units[to_multiply[0]][1] != V_BLEND or s >= max(WV_QUANT_STEPS)):
                 to_drain.extend(multiply(to_multiply[0]))
                 to_multiply = to_multiply[1:]
+            if s + SCALE_LEAD in needs_scaling:
+                scale_now(s + SCALE_LEAD)
             if s <= last:
-                group_rows(s, "scalar")
-            convert_wv(s, "scalar")
-            if s < len(units) + QUANT_LAG - 1:
-                for entry in to_drain[: DRAINS[s]]:
-                    drain(entry, "scalar")
-                to_drain = to_drain[DRAINS[s] :]
-                for entry in to_drain[: VECTOR_DRAINS.get(s, 0)]:
-                    drain(entry, "vector")
-                to_drain = to_drain[VECTOR_DRAINS.get(s, 0) :]
-        for n, entry in enumerate(to_drain):
-            drain(entry, "scalar" if n % 2 == 0 else "vector")
+                interleave_on_scalar(s)
+            if 0 <= s - WV_CAST_FROM < 2 * PASSES:
+                cast_wv(s - WV_CAST_FROM)
+            if s <= last:
+                for finished in to_drain[:DRAINS_PER_STEP]:
+                    drain(finished, nc.scalar.copy)
+                to_drain = to_drain[DRAINS_PER_STEP:]
+
+        for n, finished in enumerate(to_drain):
+            drain(finished, nc.vector.tensor_copy if n % 2 else nc.scalar.copy)

@@ -13,7 +13,6 @@ U8 = mybir.dt.uint8
 FP8X4 = mybir.dt.float8_e4m3fn_x4
 FP4X4 = mybir.dt.float4_e2m1fn_x4
 ALU = mybir.AluOpType
-ACT = mybir.ActivationFunctionType
 
 P = 128
 SLOTS = 4
@@ -27,14 +26,10 @@ MU_PITCH = 16
 PAD = 8
 
 CHUNKS = [256, 512, 256]
-SCALED_SLOTS = {(0, 0): 4, (1, 0): 1}
-SCALE_LEAD = 2
 QUANT_LAG = 2
-LATE_UNITS = 3
-SHARED_UNITS = 5
-SHARED_TOKENS = 128
-WV_CAST_FROM = 2
-WV_QUANT_STEPS = [5, 7]
+VECTOR_TOKENS = [128, 256]
+WV_CAST_STEPS = [1, 3, 4, 5]
+WV_QUANT_STEPS = [5, 6]
 DRAINS_PER_STEP = 3
 
 
@@ -56,7 +51,6 @@ def tile_mix_rwkv_fm_none_kernel(
         ctx.enter_context(tc.manual_schedule())
 
         mu_sb = keep.tile([P, PASSES, MU_PITCH], F32, name="mu_sb")
-        rest_sb = keep.tile([P, PASSES, MU_PITCH], F32, name="rest_sb")
         wr_codes = keep.tile([P, PASSES, 2 * M], U8, name="wr_codes", align_bytes=64)
         wk_codes = keep.tile([P, PASSES, M], U32, name="wk_codes", align_bytes=64)
         wr_plane = keep.tile([P, PASSES, M], U8, name="wr_plane", align_bytes=64)
@@ -92,10 +86,10 @@ def tile_mix_rwkv_fm_none_kernel(
         nc.vector.memset(wr_plane[:].bitcast(I32), 0)
         nc.vector.memset(wk_plane[:].bitcast(I32), 0)
 
+        load_x(0, 0, 1)
         nc.sync.dma_start(
             out=mu_sb[:, :, : BLENDS * SLOTS], in_=mu.rearrange("(a p j) i -> p a (j i)", a=PASSES, j=SLOTS)
         )
-        load_x(0, 0, 1)
         load_x(0, 1, SLOTS)
         load_wv(0)
         load_x(1, 0, SLOTS)
@@ -106,62 +100,36 @@ def tile_mix_rwkv_fm_none_kernel(
         load_x(2, 0, SLOTS)
         load_x(2, 1, SLOTS)
 
-        nc.vector.tensor_scalar(
-            out=rest_sb[:, :, : BLENDS * SLOTS],
-            in0=mu_sb[:, :, : BLENDS * SLOTS],
-            scalar1=-1.0,
-            scalar2=1.0,
-            op0=ALU.mult,
-            op1=ALU.add,
-        )
+        diff, blended, grouped, codes, planes, acc = {}, {}, {}, {}, {}, {}
 
-        diff, scaled, blended, grouped, codes, planes, acc = {}, {}, {}, {}, {}, {}, {}
-
-        def before(c, a):
-            return x_sb[c, a][:, :, PAD - 1 : PAD - 1 + CHUNKS[c]]
-
-        def now(c, a):
-            return x_sb[c, a][:, :, PAD:]
-
-        def difference(c, a):
-            first = SCALED_SLOTS.get((c, a), 0)
-            diff[c, a] = work.tile([P, SLOTS, CHUNKS[c]], F32, name="diff", tag="diff")
-            nc.vector.tensor_tensor(
-                out=diff[c, a][:, first:, :],
-                in0=before(c, a)[:, first:, :],
-                in1=now(c, a)[:, first:, :],
-                op=ALU.subtract,
-            )
-
-        def scale_now(u):
-            c, i, a = units[u]
-            slots = SCALED_SLOTS[c, a]
-            scaled[u] = work.tile([P, slots, CHUNKS[c]], F32, name="scaled", tag="scaled")
-            for j in range(slots):
-                nc.scalar.activation(
-                    out=scaled[u][:, j, :],
-                    in_=now(c, a)[:, j, :],
-                    func=ACT.Copy,
-                    scale=rest_sb[:, a, BLENDS * j + i : BLENDS * j + i + 1],
+        def difference(c, a, slots_per_call):
+            width = CHUNKS[c]
+            diff[c, a] = work.tile([P, SLOTS, width], F32, name="diff", tag="diff")
+            for j in range(0, SLOTS, slots_per_call):
+                slots = slice(j, j + slots_per_call)
+                nc.vector.tensor_tensor(
+                    out=diff[c, a][:, slots, :],
+                    in0=x_sb[c, a][:, slots, PAD - 1 : PAD - 1 + width],
+                    in1=x_sb[c, a][:, slots, PAD:],
+                    op=ALU.subtract,
                 )
 
         def blend(u):
             c, i, a = units[u]
-            first = SCALED_SLOTS.get((c, a), 0)
             blended[u] = work.tile([P, SLOTS, CHUNKS[c]], BF16, name="blended", tag="blended")
-            for j in list(range(first, SLOTS)) + list(range(first)):
-                factor, term = (before(c, a), scaled[u]) if j < first else (diff[c, a], now(c, a))
+            for j in range(SLOTS):
                 nc.vector.scalar_tensor_tensor(
                     out=blended[u][:, j, :],
-                    in0=factor[:, j, :],
+                    in0=diff[c, a][:, j, :],
                     scalar=mu_sb[:, a, BLENDS * j + i : BLENDS * j + i + 1],
-                    in1=term[:, j, :],
+                    in1=x_sb[c, a][:, j, PAD:],
                     op0=ALU.mult,
                     op1=ALU.add,
                 )
 
         def vector_tokens(u):
-            return SHARED_TOKENS if u > last - SHARED_UNITS else 0
+            first_shared = len(units) - len(VECTOR_TOKENS)
+            return VECTOR_TOKENS[u - first_shared] if u >= first_shared else 0
 
         def interleave_on_vector(u):
             cut = vector_tokens(u)
@@ -242,19 +210,17 @@ def tile_mix_rwkv_fm_none_kernel(
             rows = outs[i][nt * P : (nt + tiles) * P, starts[c] : starts[c] + width]
             nc.sync.dma_start(out=rows.rearrange("(h p) t -> p h t", p=P), in_=result[:])
 
-        needs_scaling = [u for u in range(len(units)) if (units[u][0], units[u][2]) in SCALED_SLOTS]
-        for u in range(SCALE_LEAD):
-            scale_now(u)
-
         to_multiply, to_drain = [], []
+        difference(0, 0, 1)
         for s in range(len(units) + 1):
             if s <= last:
                 blend(s)
-                grouped[s] = work.tile([P, CHUNKS[units[s][0]], SLOTS], BF16, name="grouped", tag="grouped", align_bytes=64)
+                width = CHUNKS[units[s][0]]
+                grouped[s] = work.tile([P, width, SLOTS], BF16, name="grouped", tag="grouped", align_bytes=64)
             if s < last and units[s + 1][1] == 0:
-                difference(units[s + 1][0], units[s + 1][2])
+                difference(units[s + 1][0], units[s + 1][2], SLOTS)
             for u in range(max(s - QUANT_LAG, 0), s):
-                if u not in codes and (u == s - QUANT_LAG or u > last - LATE_UNITS):
+                if u == s - QUANT_LAG or u == last:
                     quantize_unit(u)
                     to_multiply.append(u)
             if s <= last and vector_tokens(s):
@@ -265,12 +231,10 @@ def tile_mix_rwkv_fm_none_kernel(
             while to_multiply and (units[to_multiply[0]][1] != V_BLEND or s >= max(WV_QUANT_STEPS)):
                 to_drain.extend(multiply(to_multiply[0]))
                 to_multiply = to_multiply[1:]
-            if s + SCALE_LEAD in needs_scaling:
-                scale_now(s + SCALE_LEAD)
-            if s <= last:
+            if s < last:
                 interleave_on_scalar(s)
-            if 0 <= s - WV_CAST_FROM < 2 * PASSES:
-                cast_wv(s - WV_CAST_FROM)
+            if s in WV_CAST_STEPS:
+                cast_wv(WV_CAST_STEPS.index(s))
             if s <= last:
                 for finished in to_drain[:DRAINS_PER_STEP]:
                     drain(finished, nc.scalar.copy)

from contextlib import ExitStack

import concourse.mybir as mybir

K, M, T = 1024, 512, 1024
FLOPS = 3 * 2 * K * M * T

F32 = mybir.dt.float32
BF16 = mybir.dt.bfloat16
I32 = mybir.dt.int32
U32 = mybir.dt.uint32
U8 = mybir.dt.uint8
FP8X4 = mybir.dt.float8_e4m3fn_x4
FP4X4 = mybir.dt.float4_e2m1fn_x4
ALU = mybir.AluOpType

P = 128
SLOTS = 4
K_PASS = P * SLOTS
PASSES = K // K_PASS
BLENDS = 3
V_BLEND = 2
N_TILES = M // P
BANK = 512
MU_PITCH = 16
PAD = 8

CHUNKS = [256, 512, 256]
QUANT_LAG = 2
VECTOR_TOKENS = [128, 256]
WV_CAST_STEPS = [1, 3, 4, 5]
WV_QUANT_STEPS = [5, 6]
DRAINS_PER_STEP = 3


def tile_mix_rwkv_fm_none_kernel(
    tc, x, mu, wr_words, wr_scales, wk_words, wk_scales, wv, out_0, out_1, out_2
):
    nc = tc.nc
    outs = [out_0, out_1, out_2]
    starts = [sum(CHUNKS[:c]) for c in range(len(CHUNKS))]

    units = [(0, i, a) for a in range(PASSES) for i in range(BLENDS)]
    units.extend((c, i, a) for c in range(1, len(CHUNKS)) for i in range(BLENDS) for a in range(PASSES))
    last = len(units) - 1

    with ExitStack() as ctx:
        keep = ctx.enter_context(tc.tile_pool(name="keep", bufs=1))
        work = ctx.enter_context(tc.tile_pool(name="work", bufs=4))
        psum = ctx.enter_context(tc.psum_pool(name="psum", bufs=8))
        ctx.enter_context(tc.manual_schedule())

        mu_sb = keep.tile([P, PASSES, MU_PITCH], F32, name="mu_sb")
        wr_codes = keep.tile([P, PASSES, 2 * M], U8, name="wr_codes", align_bytes=64)
        wk_codes = keep.tile([P, PASSES, M], U32, name="wk_codes", align_bytes=64)
        wr_plane = keep.tile([P, PASSES, M], U8, name="wr_plane", align_bytes=64)
        wk_plane = keep.tile([P, PASSES, M], U8, name="wk_plane", align_bytes=64)
        wv_rows = [keep.tile([P, SLOTS, M], F32, name="wv_rows%d" % a) for a in range(PASSES)]
        wv_grouped = [keep.tile([P, M, SLOTS], BF16, name="wv_grouped%d" % a, align_bytes=64) for a in range(PASSES)]
        wv_codes = [keep.tile([P, M], U32, name="wv_codes%d" % a, align_bytes=64) for a in range(PASSES)]
        wv_plane = [keep.tile([P, M], U8, name="wv_plane%d" % a, align_bytes=64) for a in range(PASSES)]
        x_sb = {}
        for c, width in enumerate(CHUNKS):
            for a in range(PASSES):
                x_sb[c, a] = keep.tile([P, SLOTS, PAD + width], F32, name="x%d_%d" % (c, a))

        def load_x(c, a, slots_per_dma):
            rows = x[a * K_PASS : (a + 1) * K_PASS, starts[c] : starts[c] + CHUNKS[c] + 1]
            rows = rows.rearrange("(p j) t -> p j t", j=SLOTS)
            for j in range(0, SLOTS, slots_per_dma):
                slots = slice(j, j + slots_per_dma)
                nc.sync.dma_start(out=x_sb[c, a][:, slots, PAD - 1 :], in_=rows[:, slots, :])

        def load_wv(a):
            rows = wv[a * K_PASS : (a + 1) * K_PASS, :]
            nc.sync.dma_start(out=wv_rows[a][:], in_=rows.rearrange("(p j) n -> p j n", j=SLOTS))

        def load_packed(codes_sb, words, plane, scale_rows):
            nc.sync.dma_start(out=codes_sb[:].bitcast(I32), in_=words.bitcast(I32))
            for r in range(4):
                nc.sync.dma_start(
                    out=plane[:].bitcast(I32)[r:P:32, :, :],
                    in_=scale_rows.bitcast(I32)[:, r:16:4, :].rearrange("a q n -> q a n"),
                )

        nc.vector.memset(wr_plane[:].bitcast(I32), 0)
        nc.vector.memset(wk_plane[:].bitcast(I32), 0)

        load_x(0, 0, 1)
        nc.sync.dma_start(
            out=mu_sb[:, :, : BLENDS * SLOTS], in_=mu.rearrange("(a p j) i -> p a (j i)", a=PASSES, j=SLOTS)
        )
        load_x(0, 1, SLOTS)
        load_wv(0)
        load_x(1, 0, SLOTS)
        load_wv(1)
        load_packed(wr_codes, wr_words.rearrange("a p b -> p a b"), wr_plane, wr_scales)
        load_x(1, 1, SLOTS)
        load_packed(wk_codes, wk_words.rearrange("a p n i -> p a (n i)"), wk_plane, wk_scales)
        load_x(2, 0, SLOTS)
        load_x(2, 1, SLOTS)

        diff, blended, grouped, codes, planes, acc = {}, {}, {}, {}, {}, {}

        def difference(c, a, slots_per_call):
            width = CHUNKS[c]
            diff[c, a] = work.tile([P, SLOTS, width], F32, name="diff", tag="diff")
            for j in range(0, SLOTS, slots_per_call):
                slots = slice(j, j + slots_per_call)
                nc.vector.tensor_tensor(
                    out=diff[c, a][:, slots, :],
                    in0=x_sb[c, a][:, slots, PAD - 1 : PAD - 1 + width],
                    in1=x_sb[c, a][:, slots, PAD:],
                    op=ALU.subtract,
                )

        def blend(u):
            c, i, a = units[u]
            blended[u] = work.tile([P, SLOTS, CHUNKS[c]], BF16, name="blended", tag="blended")
            for j in range(SLOTS):
                nc.vector.scalar_tensor_tensor(
                    out=blended[u][:, j, :],
                    in0=diff[c, a][:, j, :],
                    scalar=mu_sb[:, a, BLENDS * j + i : BLENDS * j + i + 1],
                    in1=x_sb[c, a][:, j, PAD:],
                    op0=ALU.mult,
                    op1=ALU.add,
                )

        def vector_tokens(u):
            first_shared = len(units) - len(VECTOR_TOKENS)
            return VECTOR_TOKENS[u - first_shared] if u >= first_shared else 0

        def interleave_on_vector(u):
            cut = vector_tokens(u)
            nc.vector.tensor_copy(out=grouped[u][:, :cut, :], in_=blended[u][:, :, :cut].rearrange("p j t -> p t j"))

        def interleave_on_scalar(u):
            cut = vector_tokens(u)
            nc.scalar.copy(
                out=grouped[u][:, cut:, :].rearrange("p (g t) j -> p g j t", t=4),
                in_=blended[u][:, :, cut:].rearrange("p j (g t) -> p g j t", t=4),
            )

        def cast_wv(piece):
            a, half = divmod(piece, 2)
            cols = slice(half * M // 2, (half + 1) * M // 2)
            nc.scalar.copy(out=wv_grouped[a][:, cols, :], in_=wv_rows[a][:, :, cols].rearrange("p j n -> p n j"))

        def quantize(codes_out, plane_out, source):
            nc.vector.quantize_mx(
                out=codes_out[:].bitcast(FP8X4), scales=plane_out[:], in_=source[:].rearrange("p t j -> p (t j)")
            )

        def quantize_unit(u):
            width = CHUNKS[units[u][0]]
            codes[u] = work.tile([P, width], U32, name="codes", tag="codes", bufs=10, align_bytes=64)
            planes[u] = work.tile([P, width], U8, name="plane", tag="plane", bufs=10, align_bytes=64)
            quantize(codes[u], planes[u], grouped[u])

        def weight(i, a, nt):
            cols = slice(nt * P, (nt + 1) * P)
            if i == 0:
                return wr_codes[:, a, 2 * nt * P : 2 * (nt + 1) * P].bitcast(FP4X4), wr_plane[:, a, cols]
            if i == 1:
                return wk_codes[:, a, cols].bitcast(FP8X4), wk_plane[:, a, cols]
            return wv_codes[a][:, cols].bitcast(FP8X4), wv_plane[a][:, cols]

        def one_pass(u, nt, sums, cols):
            c, i, a = units[u]
            w_codes, w_plane = weight(i, a, nt)
            nc.tensor.matmul_mx(
                out=sums,
                lhsT=w_codes,
                lhsT_scale=w_plane,
                rhs=codes[u][:, cols].bitcast(FP8X4),
                rhs_scale=planes[u][:, cols],
                start=(a == 0),
                stop=(a == PASSES - 1),
            )

        def multiply(u):
            c, i, a = units[u]
            width = CHUNKS[c]
            if (c, i) == units[last][:2]:
                for nt in range(N_TILES):
                    if a == 0:
                        acc[c, i, nt] = psum.tile([P, BANK], F32, name="acc", tag="acc")
                    one_pass(u, nt, acc[c, i, nt][:, :width], slice(0, width))
                return [(c, i, nt, 1) for nt in range(N_TILES)] if a == PASSES - 1 else []
            if a < PASSES - 1:
                return []
            per_bank = BANK // width
            n_cols = P if i == 0 and width < BANK else width
            for nt in range(N_TILES):
                if nt % per_bank == 0:
                    acc[c, i, nt] = psum.tile([P, BANK], F32, name="acc", tag="acc")
                bank = acc[c, i, nt - nt % per_bank]
                for t0 in range(0, width, n_cols):
                    at = (nt % per_bank) * width + t0
                    for b in range(PASSES):
                        one_pass(units.index((c, i, b)), nt, bank[:, at : at + n_cols], slice(t0, t0 + n_cols))
            return [(c, i, nt, per_bank) for nt in range(0, N_TILES, per_bank)]

        def drain(finished, copy):
            c, i, nt, tiles = finished
            width = CHUNKS[c]
            result = work.tile([P, tiles, width], F32, name="result", tag="result", bufs=12)
            copy(out=result[:], in_=acc[c, i, nt][:, : tiles * width].rearrange("p (h t) -> p h t", h=tiles))
            rows = outs[i][nt * P : (nt + tiles) * P, starts[c] : starts[c] + width]
            nc.sync.dma_start(out=rows.rearrange("(h p) t -> p h t", p=P), in_=result[:])

        to_multiply, to_drain = [], []
        difference(0, 0, 1)
        for s in range(len(units) + 1):
            if s <= last:
                blend(s)
                width = CHUNKS[units[s][0]]
                grouped[s] = work.tile([P, width, SLOTS], BF16, name="grouped", tag="grouped", align_bytes=64)
            if s < last and units[s + 1][1] == 0:
                difference(units[s + 1][0], units[s + 1][2], SLOTS)
            for u in range(max(s - QUANT_LAG, 0), s):
                if u == s - QUANT_LAG or u == last:
                    quantize_unit(u)
                    to_multiply.append(u)
            if s <= last and vector_tokens(s):
                interleave_on_vector(s)
            if s in WV_QUANT_STEPS:
                a = WV_QUANT_STEPS.index(s)
                quantize(wv_codes[a], wv_plane[a], wv_grouped[a])
            while to_multiply and (units[to_multiply[0]][1] != V_BLEND or s >= max(WV_QUANT_STEPS)):
                to_drain.extend(multiply(to_multiply[0]))
                to_multiply = to_multiply[1:]
            if s < last:
                interleave_on_scalar(s)
            if s in WV_CAST_STEPS:
                cast_wv(WV_CAST_STEPS.index(s))
            if s <= last:
                for finished in to_drain[:DRAINS_PER_STEP]:
                    drain(finished, nc.scalar.copy)
                to_drain = to_drain[DRAINS_PER_STEP:]

        for n, finished in enumerate(to_drain):
            drain(finished, nc.vector.tensor_copy if n % 2 else nc.scalar.copy)
